import numpy as np
import ml_dtypes

BF16 = ml_dtypes.bfloat16


def bf(x):
    return np.asarray(x, np.float32).astype(BF16)


def f32(x):
    return np.asarray(x, np.float32)


def f64(x):
    return np.asarray(x).astype(np.float64)


def striped(idx):
    return np.tile(idx.reshape(-1, 16).T, (8, 1))


def rows(idx, k):
    return np.tile(idx, (k, 1))


def look(tab, idx):
    return np.take_along_axis(f64(tab), rows(idx, len(tab)), axis=1)


K, S, H, D, V, N = 128, 2048, 256, 2, 1024, 2048


def setup_inputs():
    return {"z": bf(np.random.standard_normal((H, S))), "wt": bf(np.random.standard_normal((H, K)) / np.sqrt(H)), "u0": f32(np.random.uniform(0.2, 1.0, (K, V))), "u1": f32(np.random.uniform(0.2, 1.0, (K, V))), "offs": striped(np.random.permutation(S)[:N])}


def reference(z, wt, u0, u1, offs):
    idx = offs[:16].T.reshape(-1)
    tab = f64(wt).T @ f64(z)
    x = f64(u0) * look(tab, idx[:V]) + f64(u1) * look(tab, idx[1 * V:2 * V])
    return x

@@ -1,0 +1,63 @@
+import concourse.mybir as mybir
+
+BF16, F32, U16 = mybir.dt.bfloat16, mybir.dt.float32, mybir.dt.uint16
+MULT, ADD = mybir.AluOpType.mult, mybir.AluOpType.add
+
+P = 128
+K_PARTS = 2
+PLACES = 2048
+PICKS = 1024
+BANK = 512
+PIECE = 512
+PER_COLUMN = 16
+
+FLOPS = 2 * P * K_PARTS * P * PLACES + 3 * P * PICKS
+
+
+def tile_lookup_pjmix_out_kernel(tc, z, wt, u0, u1, offs, out):
+    nc = tc.nc
+    with (
+        tc.tile_pool(name="held", bufs=1) as held,
+        tc.tile_pool(name="ring", bufs=2) as ring,
+        tc.psum_pool(name="banks", bufs=4) as banks,
+    ):
+        weights = held.tile([P, K_PARTS, P], BF16)
+        nc.scalar.dma_start(weights[:], wt.rearrange("(p k) r -> p k r", k=K_PARTS))
+        features = held.tile([P, K_PARTS, PLACES], BF16)
+        z_rows = z.rearrange("(p k) n -> p k n", k=K_PARTS)
+        for start in range(0, PLACES, BANK):
+            cols = slice(start, start + BANK)
+            nc.sync.dma_start(features[:, :, cols], z_rows[:, :, cols])
+        offsets = held.tile([P, 2 * PICKS // PER_COLUMN], U16)
+        nc.sync.dma_start(offsets[:], offs)
+        scale0 = held.tile([P, PICKS], F32)
+        nc.sync.dma_start(scale0[:], u0)
+        scale1 = held.tile([P, PICKS], F32)
+        nc.sync.dma_start(scale1[:], u1)
+
+        table = held.tile([P, PLACES], F32)
+        for block in range(PLACES // BANK):
+            cols = slice(block * BANK, (block + 1) * BANK)
+            bank = banks.tile([P, BANK], F32)
+            for k in range(K_PARTS):
+                nc.tensor.matmul(
+                    bank[:], weights[:, k, :], features[:, k, cols],
+                    start=(k == 0), stop=(k == K_PARTS - 1),
+                )
+            if block % 2 == 0:
+                nc.scalar.copy(table[:, cols], bank[:])
+            else:
+                nc.vector.tensor_copy(table[:, cols], bank[:])
+
+        for start in range(0, PICKS, PIECE):
+            cols = slice(start, start + PIECE)
+            products = []
+            for part, scale in enumerate((scale0, scale1)):
+                first = (part * PICKS + start) // PER_COLUMN
+                entries = offsets[:, first : first + PIECE // PER_COLUMN]
+                product = ring.tile([P, PIECE], F32, name=f"product{part}")
+                nc.vector.tensor_tensor(product[:], table[:].indirect(entries), scale[:, cols], MULT)
+                products.append(product)
+            total = ring.tile([P, PIECE], F32)
+            nc.vector.tensor_tensor(total[:], products[0][:], products[1][:], ADD)
+            nc.sync.dma_start(out[:, cols], total[:])

@@ -1,4 +1,5 @@
 import concourse.mybir as mybir
+from concourse.masks import make_identity
 
 BF16, F32, U16 = mybir.dt.bfloat16, mybir.dt.float32, mybir.dt.uint16
 MULT, ADD = mybir.AluOpType.mult, mybir.AluOpType.add
@@ -7,8 +8,10 @@ P = 128
 K_PARTS = 2
 PLACES = 2048
 PICKS = 1024
-BANK = 512
-PIECE = 512
+BLOCK = 256
+LOAD = 512
+WARM_UPS = 3
+PIECES = (512, 256, 256)
 PER_COLUMN = 16
 
 FLOPS = 2 * P * K_PARTS * P * PLACES + 3 * P * PICKS
@@ -18,27 +21,40 @@ def tile_lookup_pjmix_out_kernel(tc, z, wt, u0, u1, offs, out):
     nc = tc.nc
     with (
         tc.tile_pool(name="held", bufs=1) as held,
-        tc.tile_pool(name="ring", bufs=2) as ring,
-        tc.psum_pool(name="banks", bufs=4) as banks,
+        tc.tile_pool(name="pieces", bufs=len(PIECES)) as pieces,
+        tc.psum_pool(name="banks", bufs=5) as banks,
+        tc.psum_pool(name="spare", bufs=1) as spare,
+        tc.psum_pool(name="sums", bufs=2) as sums,
     ):
         weights = held.tile([P, K_PARTS, P], BF16)
         nc.scalar.dma_start(weights[:], wt.rearrange("(p k) r -> p k r", k=K_PARTS))
         features = held.tile([P, K_PARTS, PLACES], BF16)
         z_rows = z.rearrange("(p k) n -> p k n", k=K_PARTS)
-        for start in range(0, PLACES, BANK):
-            cols = slice(start, start + BANK)
+        for start in range(0, PLACES, LOAD):
+            cols = slice(start, start + LOAD)
             nc.sync.dma_start(features[:, :, cols], z_rows[:, :, cols])
         offsets = held.tile([P, 2 * PICKS // PER_COLUMN], U16)
         nc.sync.dma_start(offsets[:], offs)
         scale0 = held.tile([P, PICKS], F32)
-        nc.sync.dma_start(scale0[:], u0)
         scale1 = held.tile([P, PICKS], F32)
-        nc.sync.dma_start(scale1[:], u1)
+        for start in range(0, PICKS, LOAD):
+            cols = slice(start, start + LOAD)
+            nc.sync.dma_start(scale0[:, cols], u0[:, cols])
+            nc.sync.dma_start(scale1[:, cols], u1[:, cols])
+
+        identity = held.tile([P, P], F32)
+        make_identity(nc, identity[:])
+
+        zeros = held.tile([P, LOAD], BF16)
+        nc.vector.memset(zeros[:], 0.0)
+        idle = spare.tile([P, LOAD], F32)
+        for warm_up in range(WARM_UPS):
+            nc.tensor.matmul(idle[:], zeros[:, :P], zeros[:], start=True, stop=True)
 
         table = held.tile([P, PLACES], F32)
-        for block in range(PLACES // BANK):
-            cols = slice(block * BANK, (block + 1) * BANK)
-            bank = banks.tile([P, BANK], F32)
+        for block in range(PLACES // BLOCK):
+            cols = slice(block * BLOCK, (block + 1) * BLOCK)
+            bank = banks.tile([P, BLOCK], F32)
             for k in range(K_PARTS):
                 nc.tensor.matmul(
                     bank[:], weights[:, k, :], features[:, k, cols],
@@ -49,15 +65,26 @@ def tile_lookup_pjmix_out_kernel(tc, z, wt, u0, u1, offs, out):
             else:
                 nc.vector.tensor_copy(table[:, cols], bank[:])
 
-        for start in range(0, PICKS, PIECE):
-            cols = slice(start, start + PIECE)
+        start = 0
+        for number, width in enumerate(PIECES):
+            cols = slice(start, start + width)
             products = []
             for part, scale in enumerate((scale0, scale1)):
                 first = (part * PICKS + start) // PER_COLUMN
-                entries = offsets[:, first : first + PIECE // PER_COLUMN]
-                product = ring.tile([P, PIECE], F32, name=f"product{part}")
+                entries = offsets[:, first : first + width // PER_COLUMN]
+                product = pieces.tile([P, width], F32, name=f"product{part}")
                 nc.vector.tensor_tensor(product[:], table[:].indirect(entries), scale[:, cols], MULT)
                 products.append(product)
-            total = ring.tile([P, PIECE], F32)
-            nc.vector.tensor_tensor(total[:], products[0][:], products[1][:], ADD)
+            total = pieces.tile([P, width], F32)
+            if number == 0:
+                bank_sum = sums.tile([P, width], F32)
+                for part, product in enumerate(products):
+                    nc.tensor.matmul(
+                        bank_sum[:], identity[:], product[:],
+                        start=(part == 0), stop=(part == 1),
+                    )
+                nc.scalar.copy(total[:], bank_sum[:])
+            else:
+                nc.vector.tensor_tensor(total[:], products[0][:], products[1][:], ADD)
             nc.sync.dma_start(out[:, cols], total[:])
+            start += width

@@ -8,8 +8,8 @@ P = 128
 K_PARTS = 2
 PLACES = 2048
 PICKS = 1024
-BLOCK = 256
-LOAD = 512
+HALF = 512
+LOADS = (512, 512, 512, 256, 256)
 WARM_UPS = 3
 PIECES = (512, 256, 256)
 PER_COLUMN = 16
@@ -30,40 +30,42 @@ def tile_lookup_pjmix_out_kernel(tc, z, wt, u0, u1, offs, out):
         nc.scalar.dma_start(weights[:], wt.rearrange("(p k) r -> p k r", k=K_PARTS))
         features = held.tile([P, K_PARTS, PLACES], BF16)
         z_rows = z.rearrange("(p k) n -> p k n", k=K_PARTS)
-        for start in range(0, PLACES, LOAD):
-            cols = slice(start, start + LOAD)
+        start = 0
+        for width in LOADS:
+            cols = slice(start, start + width)
             nc.sync.dma_start(features[:, :, cols], z_rows[:, :, cols])
+            start += width
         offsets = held.tile([P, 2 * PICKS // PER_COLUMN], U16)
         nc.sync.dma_start(offsets[:], offs)
         scale0 = held.tile([P, PICKS], F32)
         scale1 = held.tile([P, PICKS], F32)
-        for start in range(0, PICKS, LOAD):
-            cols = slice(start, start + LOAD)
+        for start in range(0, PICKS, HALF):
+            cols = slice(start, start + HALF)
             nc.sync.dma_start(scale0[:, cols], u0[:, cols])
             nc.sync.dma_start(scale1[:, cols], u1[:, cols])
 
         identity = held.tile([P, P], F32)
         make_identity(nc, identity[:])
 
-        zeros = held.tile([P, LOAD], BF16)
+        zeros = held.tile([P, HALF], BF16)
         nc.vector.memset(zeros[:], 0.0)
-        idle = spare.tile([P, LOAD], F32)
+        idle = spare.tile([P, HALF], F32)
         for warm_up in range(WARM_UPS):
             nc.tensor.matmul(idle[:], zeros[:, :P], zeros[:], start=True, stop=True)
 
         table = held.tile([P, PLACES], F32)
-        for block in range(PLACES // BLOCK):
-            cols = slice(block * BLOCK, (block + 1) * BLOCK)
-            bank = banks.tile([P, BLOCK], F32)
-            for k in range(K_PARTS):
-                nc.tensor.matmul(
-                    bank[:], weights[:, k, :], features[:, k, cols],
-                    start=(k == 0), stop=(k == K_PARTS - 1),
-                )
-            if block % 2 == 0:
-                nc.scalar.copy(table[:, cols], bank[:])
-            else:
-                nc.vector.tensor_copy(table[:, cols], bank[:])
+        start = 0
+        for width in LOADS:
+            for copy_out in (nc.scalar.copy, nc.vector.tensor_copy):
+                cols = slice(start, start + width // 2)
+                bank = banks.tile([P, width // 2], F32)
+                for k in range(K_PARTS):
+                    nc.tensor.matmul(
+                        bank[:], weights[:, k, :], features[:, k, cols],
+                        start=(k == 0), stop=(k == K_PARTS - 1),
+                    )
+                copy_out(table[:, cols], bank[:])
+                start += width // 2
 
         start = 0
         for number, width in enumerate(PIECES):
@@ -84,7 +86,8 @@ def tile_lookup_pjmix_out_kernel(tc, z, wt, u0, u1, offs, out):
                         start=(part == 0), stop=(part == 1),
                     )
                 nc.scalar.copy(total[:], bank_sum[:])
+                nc.scalar.dma_start(out[:, cols], total[:])
             else:
                 nc.vector.tensor_tensor(total[:], products[0][:], products[1][:], ADD)
-            nc.sync.dma_start(out[:, cols], total[:])
+                nc.sync.dma_start(out[:, cols], total[:])
             start += width

import concourse.mybir as mybir
from concourse.masks import make_identity

BF16, F32, U16 = mybir.dt.bfloat16, mybir.dt.float32, mybir.dt.uint16
MULT, ADD = mybir.AluOpType.mult, mybir.AluOpType.add

P = 128
K_PARTS = 2
PLACES = 2048
PICKS = 1024
HALF = 512
LOADS = (512, 512, 512, 256, 256)
WARM_UPS = 3
PIECES = (512, 256, 256)
PER_COLUMN = 16

FLOPS = 2 * P * K_PARTS * P * PLACES + 3 * P * PICKS


def tile_lookup_pjmix_out_kernel(tc, z, wt, u0, u1, offs, out):
    nc = tc.nc
    with (
        tc.tile_pool(name="held", bufs=1) as held,
        tc.tile_pool(name="pieces", bufs=len(PIECES)) as pieces,
        tc.psum_pool(name="banks", bufs=5) as banks,
        tc.psum_pool(name="spare", bufs=1) as spare,
        tc.psum_pool(name="sums", bufs=2) as sums,
    ):
        weights = held.tile([P, K_PARTS, P], BF16)
        nc.scalar.dma_start(weights[:], wt.rearrange("(p k) r -> p k r", k=K_PARTS))
        features = held.tile([P, K_PARTS, PLACES], BF16)
        z_rows = z.rearrange("(p k) n -> p k n", k=K_PARTS)
        start = 0
        for width in LOADS:
            cols = slice(start, start + width)
            nc.sync.dma_start(features[:, :, cols], z_rows[:, :, cols])
            start += width
        offsets = held.tile([P, 2 * PICKS // PER_COLUMN], U16)
        nc.sync.dma_start(offsets[:], offs)
        scale0 = held.tile([P, PICKS], F32)
        scale1 = held.tile([P, PICKS], F32)
        for start in range(0, PICKS, HALF):
            cols = slice(start, start + HALF)
            nc.sync.dma_start(scale0[:, cols], u0[:, cols])
            nc.sync.dma_start(scale1[:, cols], u1[:, cols])

        identity = held.tile([P, P], F32)
        make_identity(nc, identity[:])

        zeros = held.tile([P, HALF], BF16)
        nc.vector.memset(zeros[:], 0.0)
        idle = spare.tile([P, HALF], F32)
        for warm_up in range(WARM_UPS):
            nc.tensor.matmul(idle[:], zeros[:, :P], zeros[:], start=True, stop=True)

        table = held.tile([P, PLACES], F32)
        start = 0
        for width in LOADS:
            for copy_out in (nc.scalar.copy, nc.vector.tensor_copy):
                cols = slice(start, start + width // 2)
                bank = banks.tile([P, width // 2], F32)
                for k in range(K_PARTS):
                    nc.tensor.matmul(
                        bank[:], weights[:, k, :], features[:, k, cols],
                        start=(k == 0), stop=(k == K_PARTS - 1),
                    )
                copy_out(table[:, cols], bank[:])
                start += width // 2

        start = 0
        for number, width in enumerate(PIECES):
            cols = slice(start, start + width)
            products = []
            for part, scale in enumerate((scale0, scale1)):
                first = (part * PICKS + start) // PER_COLUMN
                entries = offsets[:, first : first + width // PER_COLUMN]
                product = pieces.tile([P, width], F32, name=f"product{part}")
                nc.vector.tensor_tensor(product[:], table[:].indirect(entries), scale[:, cols], MULT)
                products.append(product)
            total = pieces.tile([P, width], F32)
            if number == 0:
                bank_sum = sums.tile([P, width], F32)
                for part, product in enumerate(products):
                    nc.tensor.matmul(
                        bank_sum[:], identity[:], product[:],
                        start=(part == 0), stop=(part == 1),
                    )
                nc.scalar.copy(total[:], bank_sum[:])
                nc.scalar.dma_start(out[:, cols], total[:])
            else:
                nc.vector.tensor_tensor(total[:], products[0][:], products[1][:], ADD)
                nc.sync.dma_start(out[:, cols], total[:])
            start += width
